import numpy as np
import ml_dtypes


def mxq(x, axis, fmt="e4m3"):
    dtype, down = {"e4m3": (ml_dtypes.float8_e4m3fn, 7), "e5m2": (ml_dtypes.float8_e5m2, 14)}[fmt]
    v = np.moveaxis(np.asarray(x, np.float32).astype(ml_dtypes.bfloat16).astype(np.float64), axis, -1)
    blocks = v.reshape(v.shape[:-1] + (-1, 32))
    amax = np.abs(blocks).max(-1, keepdims=True)
    byte = np.maximum(np.where(amax > 0, np.frexp(amax)[1] - 1 + 127, 0) - down, 1)
    scale = np.exp2(byte - 127.0)
    codes = (blocks / scale).astype(np.float32).astype(dtype).astype(np.float64)
    return np.moveaxis((codes * scale).reshape(v.shape), -1, axis)


WIDE = False


def mx_kscale(k):
    if not WIDE:
        return np.ones(k)
    levels = np.array([10, -10, 5, -5, 0])
    if k % 512:
        return np.exp2(np.random.permutation(np.resize(levels, k // 32))).repeat(32)
    a = np.empty((k // 512, 16))
    for p in range(k // 512):
        a[p, :8] = np.random.permutation(np.resize(levels, 8))
        for g in range(8):
            far = levels[np.abs(levels - a[p, g]) >= 10]
            a[p, g + 8] = far[np.random.randint(len(far))]
    return np.exp2(a.ravel()).repeat(32)


def f64(x):
    return np.asarray(x).astype(np.float64)


def striped(idx):
    return np.tile(idx.reshape(-1, 16).T, (8, 1)).astype(np.uint16)


def unstriped(offs):
    return offs[:16].T.reshape(-1).astype(np.int64)


def gelu(v):
    return 0.5 * v * (1.0 + np.tanh(np.sqrt(2.0 / np.pi) * (v + 0.044715 * v**3)))


K, T, E, C, N = 1536, 1024, 8, 256, 128


def by_expert(wq, xq):
    return np.concatenate([wq[e].T @ xq[:, e * C:(e + 1) * C] for e in range(E)], axis=1)


def setup_inputs():
    n = np.random.standard_normal
    s = mx_kscale(K)[:, None]
    first = np.random.permutation(np.repeat(np.arange(E), T // E))
    second = (first + 1 + np.random.permutation(np.repeat(np.arange(E - 1), -(-T // (E - 1)))[:T])) % E
    while np.bincount(second, minlength=E).max() != T // E:
        load = np.bincount(second, minlength=E); hi, lo = int(load.argmax()), int(load.argmin())
        t = np.flatnonzero((second == hi) & (first != lo))[0]; second[t] = lo
    slot_token = np.empty(E * C, np.int64); pos = np.empty((2, T), np.int64); fill = np.zeros(E, np.int64)
    place = np.stack([np.random.permutation(C) for _ in range(E)])
    for r, deal in enumerate((first, second)):
        for t in np.random.permutation(T):
            e = deal[t]; j = e * C + place[e, fill[e]]; fill[e] += 1; slot_token[j] = t; pos[r, t] = j
    g = np.random.uniform(0.2, 0.8, T)
    return {
        "xT": (n((K, T)) * s).astype(np.float32),
        "w": (n((E, K, N)) / np.sqrt(K) / s[None]).astype(np.float32),
        "b": (0.3 * n((N, E))).astype(np.float32),
        "gate": np.stack([np.tile(g, (N, 1)), np.tile(1.0 - g, (N, 1))]).astype(np.float32),
        "offs": striped(slot_token),
        "pos1": striped(pos[0]),
        "pos2": striped(pos[1]),
    }


def reference(xT, w, b, gate, offs, pos1, pos2):
    idx = unstriped(offs)
    xq = mxq(f64(xT)[:, idx], 0, "e4m3")
    y = by_expert(mxq(f64(w), 1, "e4m3"), xq)
    y = gelu(y + np.repeat(f64(b), C, axis=1))
    return f64(gate[0]) * y[:, unstriped(pos1)] + f64(gate[1]) * y[:, unstriped(pos2)]

@@ -1,0 +1,138 @@
+from contextlib import ExitStack
+
+import concourse.mybir as mybir
+
+K, T, E, C, N = 1536, 1024, 8, 256, 128
+P = 128
+PACK = 4
+A = K // (P * PACK)
+G = E * A
+S = E * C
+
+F32 = mybir.dt.float32
+BF16 = mybir.dt.bfloat16
+U32 = mybir.dt.uint32
+U16 = mybir.dt.uint16
+U8 = mybir.dt.uint8
+FP8X4 = mybir.dt.float8_e4m3fn_x4
+MULT = mybir.AluOpType.mult
+GELU = mybir.ActivationFunctionType.Gelu_apprx_tanh
+
+FLOPS = 2 * S * K * N
+
+GATHER_CUTS = (0, 768, 1536, 2048)
+TOKEN_CUTS = (0, 512, 768, 1024)
+W_CUTS = (0, 4, 8, 12, 16, 20, 24)
+
+
+def tile_routed_moe_kernel(tc, xT, w, b, gate, offs, pos1, pos2, out):
+    nc = tc.nc
+    x_view = xT.rearrange("(a p t) n -> a p t n", p=P, t=PACK)
+    w_view = w.flatten_outer_dims().rearrange("(g p t) n -> p g (t n)", p=P, t=PACK)
+
+    with ExitStack() as ctx:
+        keep = ctx.enter_context(tc.tile_pool(name="keep", bufs=1))
+        psum = ctx.enter_context(tc.psum_pool(name="psum", bufs=1))
+
+        offs_t = keep.tile([P, S // 16], U16, name="offs_t")
+        pos_t = [keep.tile([P, T // 16], U16, name=f"pos_t{i}") for i in range(2)]
+        x_codes = [keep.tile([P, T], U32, name=f"x_codes{a}", align_bytes=64) for a in range(A)]
+        x_bytes = keep.tile([P, T], U8, name="x_bytes", align_bytes=64)
+        g_codes = [keep.tile([P, S], U32, name=f"g_codes{a}", align_bytes=64) for a in range(A)]
+        g_bytes = keep.tile([P, S], U8, name="g_bytes", align_bytes=64)
+        w_codes = keep.tile([P, G * N], U32, name="w_codes", align_bytes=64)
+        w_bytes = keep.tile([P, G * N], U8, name="w_bytes", align_bytes=64)
+        bias = keep.tile([P, E], F32, name="bias")
+        gates = [keep.tile([P, T], F32, name=f"gates{i}") for i in range(2)]
+        warm = keep.tile([P, 16], F32, name="warm")
+        acc = [psum.tile([P, C], F32, name=f"acc{e}") for e in range(E)]
+
+        x_chunks = []
+        for a in range(A):
+            width = 256 if a == 0 else 512
+            for t0 in range(0, T, width):
+                raw = keep.tile([P, PACK, width], F32, name=f"x_raw{a}_{t0}")
+                nc.sync.dma_start(raw[:], x_view[a, :, :, t0 : t0 + width])
+                x_chunks.append((a, t0, width, raw))
+            if a == 0:
+                nc.sync.dma_start(offs_t[:], offs)
+        nc.sync.dma_start(bias[:], b)
+        w_raws = []
+        for g0, g1 in zip(W_CUTS[:-1], W_CUTS[1:]):
+            raw = keep.tile([P, g1 - g0, PACK, N], F32, name=f"w_raw{g0}", tag="tail" if g1 == G else "")
+            nc.sync.dma_start(raw[:].rearrange("p g t n -> p g (t n)"), w_view[:, g0:g1, :])
+            w_raws.append(raw)
+        nc.sync.dma_start(pos_t[0][:], pos1)
+        nc.sync.dma_start(pos_t[1][:], pos2)
+        for i in range(2):
+            nc.sync.dma_start(gates[i][:], gate[i])
+
+        nc.gpsimd.memset(x_bytes[:], 0)
+        nc.vector.memset(warm[:], 0.0)
+        nc.scalar.activation(warm[:, 8:9], warm[:, 0:1], GELU)
+
+        def spread(copy, grouped, raw, n0, n1):
+            copy(
+                grouped[:, n0:n1, :].rearrange("p (c i) t -> p c t i", i=4),
+                raw[:, :, n0:n1].rearrange("p t (c i) -> p c t i", i=4),
+            )
+
+        def gather_codes(a):
+            for s0, s1 in zip(GATHER_CUTS[:-1], GATHER_CUTS[1:]):
+                nc.vector.tensor_copy(g_codes[a][:, s0:s1], x_codes[a][:].indirect(offs_t[:, s0 // 16 : s1 // 16]))
+
+        for i, (a, t0, width, raw) in enumerate(x_chunks):
+            grouped = keep.tile([P, width, PACK], BF16, name=f"x_grouped{i}", align_bytes=64)
+            if i in (1, 3):
+                spread(nc.vector.tensor_copy, grouped, raw, 0, width)
+            else:
+                spread(nc.scalar.copy, grouped, raw, 0, width)
+            nc.vector.quantize_mx(
+                out=x_codes[a][:, t0 : t0 + width].bitcast(FP8X4),
+                scales=x_bytes[4 * a : P, t0 : t0 + width],
+                in_=grouped[:].rearrange("p n t -> p (n t)"),
+            )
+            if t0 + width == T:
+                gather_codes(a)
+
+        for j, raw in enumerate(w_raws):
+            g0, g1 = W_CUTS[j], W_CUTS[j + 1]
+            grouped = keep.tile([P, g1 - g0, N, PACK], BF16, name=f"w_grouped{g0}", align_bytes=64)
+            nc.scalar.copy(
+                grouped[:].rearrange("p g (c i) t -> p g c t i", i=4),
+                raw[:].rearrange("p g t (c i) -> p g c t i", i=4),
+            )
+            nc.vector.quantize_mx(
+                out=w_codes[:, g0 * N : g1 * N].bitcast(FP8X4),
+                scales=w_bytes[:, g0 * N : g1 * N],
+                in_=grouped[:].rearrange("p g n t -> p (g n t)"),
+            )
+            if j < len(GATHER_CUTS) - 1:
+                s0, s1 = GATHER_CUTS[j], GATHER_CUTS[j + 1]
+                nc.vector.tensor_copy(g_bytes[:, s0:s1], x_bytes[:].indirect(offs_t[:, s0 // 16 : s1 // 16]))
+
+        y = keep.tile([P, S], F32, name="y", tag="tail")
+        for e in range(E):
+            slots = slice(e * C, (e + 1) * C)
+            for a in range(A):
+                cols = slice((e * A + a) * N, (e * A + a + 1) * N)
+                nc.tensor.matmul_mx(
+                    out=acc[e][:],
+                    lhsT=w_codes[:, cols].bitcast(FP8X4),
+                    lhsT_scale=w_bytes[:, cols],
+                    rhs=g_codes[a][:, slots].bitcast(FP8X4),
+                    rhs_scale=g_bytes[4 * a : P, slots],
+                    start=(a == 0),
+                    stop=(a == A - 1),
+                )
+            nc.scalar.activation(y[:, slots], acc[e][:], GELU, bias=bias[:, e : e + 1])
+
+        for t0, t1 in zip(TOKEN_CUTS[:-1], TOKEN_CUTS[1:]):
+            parts = [keep.tile([P, t1 - t0], F32, name=f"part{i}_{t0}") for i in range(2)]
+            for i in range(2):
+                nc.vector.tensor_tensor(
+                    parts[i][:], y[:].indirect(pos_t[i][:, t0 // 16 : t1 // 16]), gates[i][:, t0:t1], MULT
+                )
+            total = keep.tile([P, t1 - t0], F32, name=f"total{t0}")
+            nc.vector.tensor_add(total[:], parts[0][:], parts[1][:])
+            nc.sync.dma_start(out[:, t0:t1], total[:])

@@ -21,8 +21,8 @@ GELU = mybir.ActivationFunctionType.Gelu_apprx_tanh
 FLOPS = 2 * S * K * N
 
 GATHER_CUTS = (0, 768, 1536, 2048)
-TOKEN_CUTS = (0, 512, 768, 1024)
-W_CUTS = (0, 4, 8, 12, 16, 20, 24)
+TOKEN_CUTS = (0, 640, 1024)
+W_CUTS = (0, 4, 8, 12, 16, 20, 22, 24)
 
 
 def tile_routed_moe_kernel(tc, xT, w, b, gate, offs, pos1, pos2, out):
@@ -38,7 +38,7 @@ def tile_routed_moe_kernel(tc, xT, w, b, gate, offs, pos1, pos2, out):
         pos_t = [keep.tile([P, T // 16], U16, name=f"pos_t{i}") for i in range(2)]
         x_codes = [keep.tile([P, T], U32, name=f"x_codes{a}", align_bytes=64) for a in range(A)]
         x_bytes = keep.tile([P, T], U8, name="x_bytes", align_bytes=64)
-        g_codes = [keep.tile([P, S], U32, name=f"g_codes{a}", align_bytes=64) for a in range(A)]
+        g_codes = [[], [], []]
         g_bytes = keep.tile([P, S], U8, name="g_bytes", align_bytes=64)
         w_codes = keep.tile([P, G * N], U32, name="w_codes", align_bytes=64)
         w_bytes = keep.tile([P, G * N], U8, name="w_bytes", align_bytes=64)
@@ -47,19 +47,18 @@ def tile_routed_moe_kernel(tc, xT, w, b, gate, offs, pos1, pos2, out):
         warm = keep.tile([P, 16], F32, name="warm")
         acc = [psum.tile([P, C], F32, name=f"acc{e}") for e in range(E)]
 
-        x_chunks = []
+        x_raws = []
         for a in range(A):
-            width = 256 if a == 0 else 512
-            for t0 in range(0, T, width):
-                raw = keep.tile([P, PACK, width], F32, name=f"x_raw{a}_{t0}")
-                nc.sync.dma_start(raw[:], x_view[a, :, :, t0 : t0 + width])
-                x_chunks.append((a, t0, width, raw))
+            for h in range(2):
+                raw = keep.tile([P, PACK, T // 2], F32, name=f"x_raw{a}_{h}")
+                nc.sync.dma_start(raw[:], x_view[a, :, :, h * T // 2 : (h + 1) * T // 2])
+                x_raws.append(raw)
             if a == 0:
                 nc.sync.dma_start(offs_t[:], offs)
         nc.sync.dma_start(bias[:], b)
         w_raws = []
         for g0, g1 in zip(W_CUTS[:-1], W_CUTS[1:]):
-            raw = keep.tile([P, g1 - g0, PACK, N], F32, name=f"w_raw{g0}", tag="tail" if g1 == G else "")
+            raw = keep.tile([P, g1 - g0, PACK, N], F32, name=f"w_raw{g0}", tag="tail" if g1 == 22 else "")
             nc.sync.dma_start(raw[:].rearrange("p g t n -> p g (t n)"), w_view[:, g0:g1, :])
             w_raws.append(raw)
         nc.sync.dma_start(pos_t[0][:], pos1)
@@ -71,34 +70,50 @@ def tile_routed_moe_kernel(tc, xT, w, b, gate, offs, pos1, pos2, out):
         nc.vector.memset(warm[:], 0.0)
         nc.scalar.activation(warm[:, 8:9], warm[:, 0:1], GELU)
 
-        def spread(copy, grouped, raw, n0, n1):
-            copy(
-                grouped[:, n0:n1, :].rearrange("p (c i) t -> p c t i", i=4),
-                raw[:, :, n0:n1].rearrange("p t (c i) -> p c t i", i=4),
-            )
+        def slots_of(i):
+            return GATHER_CUTS[i], GATHER_CUTS[i + 1]
 
-        def gather_codes(a):
-            for s0, s1 in zip(GATHER_CUTS[:-1], GATHER_CUTS[1:]):
-                nc.vector.tensor_copy(g_codes[a][:, s0:s1], x_codes[a][:].indirect(offs_t[:, s0 // 16 : s1 // 16]))
+        def gather_codes(a, i):
+            s0, s1 = slots_of(i)
+            tag = "swap%d" % (2 * i - 1) if a == 2 and i > 0 else ""
+            part = keep.tile([P, s1 - s0], U32, name=f"g_codes{a}_{i}", tag=tag, align_bytes=64)
+            nc.vector.tensor_copy(part[:], x_codes[a][:].indirect(offs_t[:, s0 // 16 : s1 // 16]))
+            g_codes[a].append(part)
 
-        for i, (a, t0, width, raw) in enumerate(x_chunks):
-            grouped = keep.tile([P, width, PACK], BF16, name=f"x_grouped{i}", align_bytes=64)
-            if i in (1, 3):
-                spread(nc.vector.tensor_copy, grouped, raw, 0, width)
-            else:
-                spread(nc.scalar.copy, grouped, raw, 0, width)
-            nc.vector.quantize_mx(
-                out=x_codes[a][:, t0 : t0 + width].bitcast(FP8X4),
-                scales=x_bytes[4 * a : P, t0 : t0 + width],
-                in_=grouped[:].rearrange("p n t -> p (n t)"),
-            )
-            if t0 + width == T:
-                gather_codes(a)
+        def gather_bytes(i):
+            s0, s1 = slots_of(i)
+            nc.vector.tensor_copy(g_bytes[:, s0:s1], x_bytes[:].indirect(offs_t[:, s0 // 16 : s1 // 16]))
+
+        for a in range(A):
+            for h in range(2):
+                raw = x_raws[2 * a + h]
+                width = 256 if a == 0 else 512
+                for n0 in range(0, 512, width):
+                    grouped = keep.tile([P, width, PACK], BF16, name=f"x_grouped{a}_{h}_{n0}", align_bytes=64)
+                    copy = nc.vector.tensor_copy if a == 0 and n0 == 256 else nc.scalar.copy
+                    copy(
+                        grouped[:].rearrange("p (c i) t -> p c t i", i=4),
+                        raw[:, :, n0 : n0 + width].rearrange("p t (c i) -> p c t i", i=4),
+                    )
+                    t0 = h * 512 + n0
+                    nc.vector.quantize_mx(
+                        out=x_codes[a][:, t0 : t0 + width].bitcast(FP8X4),
+                        scales=x_bytes[4 * a : P, t0 : t0 + width],
+                        in_=grouped[:].rearrange("p n t -> p (n t)"),
+                    )
+            if a < 2:
+                for i in range(3):
+                    gather_codes(a, i)
 
         for j, raw in enumerate(w_raws):
+            if j in (0, 2, 4):
+                gather_codes(2, j // 2)
+                gather_bytes(j // 2)
             g0, g1 = W_CUTS[j], W_CUTS[j + 1]
-            grouped = keep.tile([P, g1 - g0, N, PACK], BF16, name=f"w_grouped{g0}", align_bytes=64)
-            nc.scalar.copy(
+            tag = f"swap{j}" if j in (1, 3) else ""
+            grouped = keep.tile([P, g1 - g0, N, PACK], BF16, name=f"w_grouped{g0}", tag=tag, align_bytes=64)
+            copy = nc.vector.tensor_copy if j == 6 else nc.scalar.copy
+            copy(
                 grouped[:].rearrange("p g (c i) t -> p g c t i", i=4),
                 raw[:].rearrange("p g t (c i) -> p g c t i", i=4),
             )
@@ -107,32 +122,42 @@ def tile_routed_moe_kernel(tc, xT, w, b, gate, offs, pos1, pos2, out):
                 scales=w_bytes[:, g0 * N : g1 * N],
                 in_=grouped[:].rearrange("p g n t -> p (g n t)"),
             )
-            if j < len(GATHER_CUTS) - 1:
-                s0, s1 = GATHER_CUTS[j], GATHER_CUTS[j + 1]
-                nc.vector.tensor_copy(g_bytes[:, s0:s1], x_bytes[:].indirect(offs_t[:, s0 // 16 : s1 // 16]))
 
         y = keep.tile([P, S], F32, name="y", tag="tail")
         for e in range(E):
             slots = slice(e * C, (e + 1) * C)
+            i = min(e // 3, 2)
+            local = slice(e * C - GATHER_CUTS[i], (e + 1) * C - GATHER_CUTS[i])
             for a in range(A):
                 cols = slice((e * A + a) * N, (e * A + a + 1) * N)
                 nc.tensor.matmul_mx(
                     out=acc[e][:],
                     lhsT=w_codes[:, cols].bitcast(FP8X4),
                     lhsT_scale=w_bytes[:, cols],
-                    rhs=g_codes[a][:, slots].bitcast(FP8X4),
+                    rhs=g_codes[a][i][:, local].bitcast(FP8X4),
                     rhs_scale=g_bytes[4 * a : P, slots],
                     start=(a == 0),
                     stop=(a == A - 1),
                 )
             nc.scalar.activation(y[:, slots], acc[e][:], GELU, bias=bias[:, e : e + 1])
 
-        for t0, t1 in zip(TOKEN_CUTS[:-1], TOKEN_CUTS[1:]):
-            parts = [keep.tile([P, t1 - t0], F32, name=f"part{i}_{t0}") for i in range(2)]
-            for i in range(2):
-                nc.vector.tensor_tensor(
-                    parts[i][:], y[:].indirect(pos_t[i][:, t0 // 16 : t1 // 16]), gates[i][:, t0:t1], MULT
-                )
-            total = keep.tile([P, t1 - t0], F32, name=f"total{t0}")
-            nc.vector.tensor_add(total[:], parts[0][:], parts[1][:])
+        parts = []
+
+        def fetch(n, i):
+            t0, t1 = TOKEN_CUTS[n], TOKEN_CUTS[n + 1]
+            part = keep.tile([P, t1 - t0], F32, name=f"part{i}_{n}")
+            nc.vector.tensor_tensor(part[:], y[:].indirect(pos_t[i][:, t0 // 16 : t1 // 16]), gates[i][:, t0:t1], MULT)
+            parts.append(part)
+
+        def finish(n):
+            t0, t1 = TOKEN_CUTS[n], TOKEN_CUTS[n + 1]
+            total = keep.tile([P, t1 - t0], F32, name=f"total{n}")
+            nc.vector.tensor_add(total[:], parts[2 * n][:], parts[2 * n + 1][:])
             nc.sync.dma_start(out[:, t0:t1], total[:])
+
+        fetch(0, 0)
+        fetch(0, 1)
+        fetch(1, 0)
+        finish(0)
+        fetch(1, 1)
+        finish(1)

@@ -16,6 +16,7 @@ U16 = mybir.dt.uint16
 U8 = mybir.dt.uint8
 FP8X4 = mybir.dt.float8_e4m3fn_x4
 MULT = mybir.AluOpType.mult
+ADD = mybir.AluOpType.add
 GELU = mybir.ActivationFunctionType.Gelu_apprx_tanh
 
 FLOPS = 2 * S * K * N
@@ -58,7 +59,7 @@ def tile_routed_moe_kernel(tc, xT, w, b, gate, offs, pos1, pos2, out):
         nc.sync.dma_start(bias[:], b)
         w_raws = []
         for g0, g1 in zip(W_CUTS[:-1], W_CUTS[1:]):
-            raw = keep.tile([P, g1 - g0, PACK, N], F32, name=f"w_raw{g0}", tag="tail" if g1 == 22 else "")
+            raw = keep.tile([P, g1 - g0, PACK, N], F32, name=f"w_raw{g0}", tag="tail" if g1 == 24 else "")
             nc.sync.dma_start(raw[:].rearrange("p g t n -> p g (t n)"), w_view[:, g0:g1, :])
             w_raws.append(raw)
         nc.sync.dma_start(pos_t[0][:], pos1)
@@ -90,11 +91,14 @@ def tile_routed_moe_kernel(tc, xT, w, b, gate, offs, pos1, pos2, out):
                 width = 256 if a == 0 else 512
                 for n0 in range(0, 512, width):
                     grouped = keep.tile([P, width, PACK], BF16, name=f"x_grouped{a}_{h}_{n0}", align_bytes=64)
-                    copy = nc.vector.tensor_copy if a == 0 and n0 == 256 else nc.scalar.copy
-                    copy(
-                        grouped[:].rearrange("p (c i) t -> p c t i", i=4),
-                        raw[:, :, n0 : n0 + width].rearrange("p t (c i) -> p c t i", i=4),
-                    )
+                    cut = 0 if a == 0 and n0 == 256 else 384 if a == 1 and h == 1 else width
+                    other = nc.vector.tensor_copy if a == 0 else nc.gpsimd.tensor_copy
+                    for copy, c0, c1 in ((nc.scalar.copy, 0, cut), (other, cut, width)):
+                        if c0 < c1:
+                            copy(
+                                grouped[:, c0:c1].rearrange("p (c i) t -> p c t i", i=4),
+                                raw[:, :, n0 + c0 : n0 + c1].rearrange("p t (c i) -> p c t i", i=4),
+                            )
                     t0 = h * 512 + n0
                     nc.vector.quantize_mx(
                         out=x_codes[a][:, t0 : t0 + width].bitcast(FP8X4),
@@ -112,11 +116,21 @@ def tile_routed_moe_kernel(tc, xT, w, b, gate, offs, pos1, pos2, out):
             g0, g1 = W_CUTS[j], W_CUTS[j + 1]
             tag = f"swap{j}" if j in (1, 3) else ""
             grouped = keep.tile([P, g1 - g0, N, PACK], BF16, name=f"w_grouped{g0}", tag=tag, align_bytes=64)
-            copy = nc.vector.tensor_copy if j == 6 else nc.scalar.copy
-            copy(
-                grouped[:].rearrange("p g (c i) t -> p g c t i", i=4),
-                raw[:].rearrange("p g t (c i) -> p g c t i", i=4),
-            )
+            if j == 2:
+                for c in range(g1 - g0):
+                    nc.gpsimd.tensor_scalar(
+                        grouped[:, c].rearrange("p (c i) t -> p c t i", i=4),
+                        raw[:, c].rearrange("p t (c i) -> p c t i", i=4),
+                        1.0,
+                        0.0,
+                        MULT,
+                        ADD,
+                    )
+            else:
+                nc.scalar.copy(
+                    grouped[:].rearrange("p g (c i) t -> p g c t i", i=4),
+                    raw[:].rearrange("p g t (c i) -> p g c t i", i=4),
+                )
             nc.vector.quantize_mx(
                 out=w_codes[:, g0 * N : g1 * N].bitcast(FP8X4),
                 scales=w_bytes[:, g0 * N : g1 * N],

from contextlib import ExitStack

import concourse.mybir as mybir

K, T, E, C, N = 1536, 1024, 8, 256, 128
P = 128
PACK = 4
A = K // (P * PACK)
G = E * A
S = E * C

F32 = mybir.dt.float32
BF16 = mybir.dt.bfloat16
U32 = mybir.dt.uint32
U16 = mybir.dt.uint16
U8 = mybir.dt.uint8
FP8X4 = mybir.dt.float8_e4m3fn_x4
MULT = mybir.AluOpType.mult
ADD = mybir.AluOpType.add
GELU = mybir.ActivationFunctionType.Gelu_apprx_tanh

FLOPS = 2 * S * K * N

GATHER_CUTS = (0, 768, 1536, 2048)
TOKEN_CUTS = (0, 640, 1024)
W_CUTS = (0, 4, 8, 12, 16, 20, 22, 24)


def tile_routed_moe_kernel(tc, xT, w, b, gate, offs, pos1, pos2, out):
    nc = tc.nc
    x_view = xT.rearrange("(a p t) n -> a p t n", p=P, t=PACK)
    w_view = w.flatten_outer_dims().rearrange("(g p t) n -> p g (t n)", p=P, t=PACK)

    with ExitStack() as ctx:
        keep = ctx.enter_context(tc.tile_pool(name="keep", bufs=1))
        psum = ctx.enter_context(tc.psum_pool(name="psum", bufs=1))

        offs_t = keep.tile([P, S // 16], U16, name="offs_t")
        pos_t = [keep.tile([P, T // 16], U16, name=f"pos_t{i}") for i in range(2)]
        x_codes = [keep.tile([P, T], U32, name=f"x_codes{a}", align_bytes=64) for a in range(A)]
        x_bytes = keep.tile([P, T], U8, name="x_bytes", align_bytes=64)
        g_codes = [[], [], []]
        g_bytes = keep.tile([P, S], U8, name="g_bytes", align_bytes=64)
        w_codes = keep.tile([P, G * N], U32, name="w_codes", align_bytes=64)
        w_bytes = keep.tile([P, G * N], U8, name="w_bytes", align_bytes=64)
        bias = keep.tile([P, E], F32, name="bias")
        gates = [keep.tile([P, T], F32, name=f"gates{i}") for i in range(2)]
        warm = keep.tile([P, 16], F32, name="warm")
        acc = [psum.tile([P, C], F32, name=f"acc{e}") for e in range(E)]

        x_raws = []
        for a in range(A):
            for h in range(2):
                raw = keep.tile([P, PACK, T // 2], F32, name=f"x_raw{a}_{h}")
                nc.sync.dma_start(raw[:], x_view[a, :, :, h * T // 2 : (h + 1) * T // 2])
                x_raws.append(raw)
            if a == 0:
                nc.sync.dma_start(offs_t[:], offs)
        nc.sync.dma_start(bias[:], b)
        w_raws = []
        for g0, g1 in zip(W_CUTS[:-1], W_CUTS[1:]):
            raw = keep.tile([P, g1 - g0, PACK, N], F32, name=f"w_raw{g0}", tag="tail" if g1 == 24 else "")
            nc.sync.dma_start(raw[:].rearrange("p g t n -> p g (t n)"), w_view[:, g0:g1, :])
            w_raws.append(raw)
        nc.sync.dma_start(pos_t[0][:], pos1)
        nc.sync.dma_start(pos_t[1][:], pos2)
        for i in range(2):
            nc.sync.dma_start(gates[i][:], gate[i])

        nc.gpsimd.memset(x_bytes[:], 0)
        nc.vector.memset(warm[:], 0.0)
        nc.scalar.activation(warm[:, 8:9], warm[:, 0:1], GELU)

        def slots_of(i):
            return GATHER_CUTS[i], GATHER_CUTS[i + 1]

        def gather_codes(a, i):
            s0, s1 = slots_of(i)
            tag = "swap%d" % (2 * i - 1) if a == 2 and i > 0 else ""
            part = keep.tile([P, s1 - s0], U32, name=f"g_codes{a}_{i}", tag=tag, align_bytes=64)
            nc.vector.tensor_copy(part[:], x_codes[a][:].indirect(offs_t[:, s0 // 16 : s1 // 16]))
            g_codes[a].append(part)

        def gather_bytes(i):
            s0, s1 = slots_of(i)
            nc.vector.tensor_copy(g_bytes[:, s0:s1], x_bytes[:].indirect(offs_t[:, s0 // 16 : s1 // 16]))

        for a in range(A):
            for h in range(2):
                raw = x_raws[2 * a + h]
                width = 256 if a == 0 else 512
                for n0 in range(0, 512, width):
                    grouped = keep.tile([P, width, PACK], BF16, name=f"x_grouped{a}_{h}_{n0}", align_bytes=64)
                    cut = 0 if a == 0 and n0 == 256 else 384 if a == 1 and h == 1 else width
                    other = nc.vector.tensor_copy if a == 0 else nc.gpsimd.tensor_copy
                    for copy, c0, c1 in ((nc.scalar.copy, 0, cut), (other, cut, width)):
                        if c0 < c1:
                            copy(
                                grouped[:, c0:c1].rearrange("p (c i) t -> p c t i", i=4),
                                raw[:, :, n0 + c0 : n0 + c1].rearrange("p t (c i) -> p c t i", i=4),
                            )
                    t0 = h * 512 + n0
                    nc.vector.quantize_mx(
                        out=x_codes[a][:, t0 : t0 + width].bitcast(FP8X4),
                        scales=x_bytes[4 * a : P, t0 : t0 + width],
                        in_=grouped[:].rearrange("p n t -> p (n t)"),
                    )
            if a < 2:
                for i in range(3):
                    gather_codes(a, i)

        for j, raw in enumerate(w_raws):
            if j in (0, 2, 4):
                gather_codes(2, j // 2)
                gather_bytes(j // 2)
            g0, g1 = W_CUTS[j], W_CUTS[j + 1]
            tag = f"swap{j}" if j in (1, 3) else ""
            grouped = keep.tile([P, g1 - g0, N, PACK], BF16, name=f"w_grouped{g0}", tag=tag, align_bytes=64)
            if j == 2:
                for c in range(g1 - g0):
                    nc.gpsimd.tensor_scalar(
                        grouped[:, c].rearrange("p (c i) t -> p c t i", i=4),
                        raw[:, c].rearrange("p t (c i) -> p c t i", i=4),
                        1.0,
                        0.0,
                        MULT,
                        ADD,
                    )
            else:
                nc.scalar.copy(
                    grouped[:].rearrange("p g (c i) t -> p g c t i", i=4),
                    raw[:].rearrange("p g t (c i) -> p g c t i", i=4),
                )
            nc.vector.quantize_mx(
                out=w_codes[:, g0 * N : g1 * N].bitcast(FP8X4),
                scales=w_bytes[:, g0 * N : g1 * N],
                in_=grouped[:].rearrange("p g n t -> p (g n t)"),
            )

        y = keep.tile([P, S], F32, name="y", tag="tail")
        for e in range(E):
            slots = slice(e * C, (e + 1) * C)
            i = min(e // 3, 2)
            local = slice(e * C - GATHER_CUTS[i], (e + 1) * C - GATHER_CUTS[i])
            for a in range(A):
                cols = slice((e * A + a) * N, (e * A + a + 1) * N)
                nc.tensor.matmul_mx(
                    out=acc[e][:],
                    lhsT=w_codes[:, cols].bitcast(FP8X4),
                    lhsT_scale=w_bytes[:, cols],
                    rhs=g_codes[a][i][:, local].bitcast(FP8X4),
                    rhs_scale=g_bytes[4 * a : P, slots],
                    start=(a == 0),
                    stop=(a == A - 1),
                )
            nc.scalar.activation(y[:, slots], acc[e][:], GELU, bias=bias[:, e : e + 1])

        parts = []

        def fetch(n, i):
            t0, t1 = TOKEN_CUTS[n], TOKEN_CUTS[n + 1]
            part = keep.tile([P, t1 - t0], F32, name=f"part{i}_{n}")
            nc.vector.tensor_tensor(part[:], y[:].indirect(pos_t[i][:, t0 // 16 : t1 // 16]), gates[i][:, t0:t1], MULT)
            parts.append(part)

        def finish(n):
            t0, t1 = TOKEN_CUTS[n], TOKEN_CUTS[n + 1]
            total = keep.tile([P, t1 - t0], F32, name=f"total{n}")
            nc.vector.tensor_add(total[:], parts[2 * n][:], parts[2 * n + 1][:])
            nc.sync.dma_start(out[:, t0:t1], total[:])

        fetch(0, 0)
        fetch(0, 1)
        fetch(1, 0)
        finish(0)
        fetch(1, 1)
        finish(1)
